import numpy as np
import ml_dtypes


def mxq(x, axis, fmt="e4m3"):
    dtype, down = {"e4m3": (ml_dtypes.float8_e4m3fn, 7), "e5m2": (ml_dtypes.float8_e5m2, 14)}[fmt]
    v = np.moveaxis(np.asarray(x, np.float32).astype(ml_dtypes.bfloat16).astype(np.float64), axis, -1)
    blocks = v.reshape(v.shape[:-1] + (-1, 32))
    amax = np.abs(blocks).max(-1, keepdims=True)
    byte = np.maximum(np.where(amax > 0, np.frexp(amax)[1] - 1 + 127, 0) - down, 1)
    scale = np.exp2(byte - 127.0)
    codes = (blocks / scale).astype(np.float32).astype(dtype).astype(np.float64)
    return np.moveaxis((codes * scale).reshape(v.shape), -1, axis)


WIDE = False


def mx_kscale(k):
    if not WIDE:
        return np.ones(k)
    levels = np.array([10, -10, 5, -5, 0])
    if k % 512:
        return np.exp2(np.random.permutation(np.resize(levels, k // 32))).repeat(32)
    a = np.empty((k // 512, 16))
    for p in range(k // 512):
        a[p, :8] = np.random.permutation(np.resize(levels, 8))
        for g in range(8):
            far = levels[np.abs(levels - a[p, g]) >= 10]
            a[p, g + 8] = far[np.random.randint(len(far))]
    return np.exp2(a.ravel()).repeat(32)


def f64(x):
    return np.asarray(x).astype(np.float64)


def striped(idx):
    return np.tile(idx.reshape(-1, 16).T, (8, 1)).astype(np.uint16)


def unstriped(offs):
    return offs[:16].T.reshape(-1).astype(np.int64)


def striped8(idx):
    return np.concatenate([x.reshape(-1, 16).T for x in idx]).astype(np.uint16)


def runs(offs, k):
    lists = np.stack([offs[16 * r : 16 * r + 16].T.reshape(-1) for r in range(8)]).astype(np.int64)
    return lists[np.arange(k) % 512 // 64]


def pack_weight(w):
    k, n = w.shape
    w = f64(np.asarray(w, np.float32).astype(ml_dtypes.bfloat16)).reshape(k // 32, 32, n)
    amax = np.abs(w).max(1)
    byte = np.clip(np.where(amax > 0, np.frexp(amax)[1] - 1 + 127 - 7, 1), 1, 254)
    scaled = (w * np.exp2(127.0 - byte)[:, None, :]).reshape(k, n).astype(np.float32)
    words = np.ascontiguousarray(scaled.reshape(k // 512, 128, 4, n).transpose(0, 1, 3, 2)).astype(ml_dtypes.float8_e4m3fn).view(np.uint8)
    return words, np.ascontiguousarray(byte.astype(np.uint8).reshape(k // 512, 16, n))


def unpack_weight(words, scales):
    g, p, n, _ = words.shape
    vals = np.ascontiguousarray(words).view(ml_dtypes.float8_e4m3fn).astype(np.float64) * np.repeat(np.exp2(scales.astype(np.float64) - 127.0), 8, axis=1)[..., None]
    return vals.transpose(0, 1, 3, 2).reshape(g * 512, n)

def planes(y):
    n, m = y.shape
    v = y.astype(np.float32).astype(ml_dtypes.bfloat16).astype(np.float64).reshape(n // 32, 32, m)
    top = np.abs(v).max(1)
    byte = np.clip(np.where(top > 0, np.frexp(top)[1] - 1 + 127 - 7, 1), 1, 254)
    codes = (v * np.exp2(127.0 - byte)[:, None, :]).reshape(n, m).astype(np.float32).astype(ml_dtypes.float8_e4m3fn).view(np.uint8)
    words = codes.reshape(n // 512, 128, 4, m).transpose(0, 1, 3, 2)
    return np.ascontiguousarray(words), np.ascontiguousarray(byte.astype(np.uint8).reshape(n // 512, 16, m))


K, T, S, H = 512, 2048, 512, 512


def setup_inputs():
    n = np.random.standard_normal
    s = mx_kscale(K)[:, None]
    u = mx_kscale(S)
    packed_xT = pack_weight(n((K, T)) * s)
    return {
        "x_words": packed_xT[0],
        "x_scales": packed_xT[1],
        "wa": (n((K, H)) / np.sqrt(K) / s).astype(np.float32),
        "wb": (n((K, H)) / np.sqrt(K) / s).astype(np.float32),
        "gt": (np.random.uniform(0.5, 1.5, (S, 1)) * u[:, None]).astype(np.float32),
        "gi": (np.random.uniform(0.5, 1.5, (S, 1)) / u[:, None]).astype(np.float32),
        "offs": striped(np.random.permutation(T)[:S]),
        "two": striped(np.random.permutation(T)[:S]),
        "n1": striped8(np.stack([np.random.permutation(H) for _ in range(8)])),
        "n2": striped8(np.stack([np.random.permutation(H) for _ in range(8)])),
        "n3": striped(np.random.permutation(H)),
        "n4": striped(np.random.permutation(H)),
    }


def reference(x_words, x_scales, wa, wb, gt, gi, offs, two, n1, n2, n3, n4):
    xq = unpack_weight(x_words, x_scales)[:, unstriped(offs)]
    a = xq.T @ mxq(f64(wa), 0, "e4m3")
    x_two = unpack_weight(x_words, x_scales)[:, unstriped(two)]
    b = x_two.T @ mxq(f64(wb), 0, "e4m3")
    z = f64(gt) * (a * (np.tanh(b[np.arange(S)[:, None], runs(n1, S)] - (b[np.arange(S)[:, None], runs(n2, S)]))))
    z2 = f64(gi) * b
    cv = 0.0625 * ((mxq(z, 0, "e4m3").T @ mxq(z2, 0, "e4m3")))
    st = cv - cv[:, unstriped(n3)]
    out_0 = np.maximum(st, st[:, unstriped(n4)])
    return (out_0,) + planes(out_0)

@@ -1,0 +1,249 @@
+from contextlib import ExitStack
+
+import concourse.mybir as mybir
+
+K, T, S, H = 512, 2048, 512, 512
+FLOPS = 3 * 2 * 512 * 512 * 512
+
+F32 = mybir.dt.float32
+BF16 = mybir.dt.bfloat16
+I32 = mybir.dt.int32
+U32 = mybir.dt.uint32
+U16 = mybir.dt.uint16
+U8 = mybir.dt.uint8
+FP8X4 = mybir.dt.float8_e4m3fn_x4
+ALU = mybir.AluOpType
+ACT = mybir.ActivationFunctionType
+
+P = 128
+PACK = 4
+HALF = H // 2
+HALF_COLS = HALF // 16
+
+
+def tile_picked_momtjointbhopmx_none_po_kernel(tc, x_words, x_scales, wa, wb, gt, gi, offs, two, n1, n2, n3, n4, out_0, out_1, out_2):
+    nc = tc.nc
+    with ExitStack() as ctx:
+        keep = ctx.enter_context(tc.tile_pool(name="keep", bufs=1))
+        psum = ctx.enter_context(tc.psum_pool(name="psum", bufs=1))
+
+        def sb(name, shape, dtype, tag=None):
+            return keep.tile(shape, dtype, name=name, tag=tag or name, align_bytes=64)
+
+        def load_list(name, src):
+            t = sb(name, [P, 32], U16)
+            nc.sync.dma_start(t[:], src)
+            return t
+
+        def half_of(lst, h):
+            return lst[:, h * HALF_COLS : (h + 1) * HALF_COLS]
+
+        xs = sb("xs", [P, T], U8)
+        nc.vector.memset(xs[:].bitcast(I32), 0)
+        two_l = load_list("two_l", two)
+        offs_l = load_list("offs_l", offs)
+        for q in range(4):
+            nc.sync.dma_start(xs[32 * q : 32 * q + 4, :].bitcast(I32), x_scales[0, 4 * q : 4 * q + 4, :].bitcast(I32))
+
+        def load_w(name, w):
+            halves = []
+            for h in range(2):
+                t = sb("%s_raw%d" % (name, h), [P, PACK, HALF], F32)
+                nc.sync.dma_start(t[:], w.rearrange("(p j) c -> p j c", j=PACK)[:, :, h * HALF : (h + 1) * HALF])
+                halves.append(t)
+            return halves
+
+        wb_raw = load_w("wb", wb)
+        xw = sb("xw", [P, T], I32)
+        nc.sync.dma_start(xw[:], x_words[0].rearrange("p c r -> p (c r)").bitcast(I32))
+        wa_raw = load_w("wa", wa)
+        gi_t = sb("gi_t", [P, PACK], F32)
+        nc.sync.dma_start(gi_t[:], gi.rearrange("(p t) o -> p (t o)", t=PACK))
+        n1_l = load_list("n1_l", n1)
+        n2_l = load_list("n2_l", n2)
+        gt_t = sb("gt_t", [P, PACK], F32)
+        nc.sync.dma_start(gt_t[:], gt.rearrange("(p t) o -> p (t o)", t=PACK))
+        n3_l = load_list("n3_l", n3)
+        n4_l = load_list("n4_l", n4)
+
+        def pick_scales(name, lst):
+            g = sb(name + "_sg", [P, S], U8)
+            nc.vector.tensor_copy(g[:], xs[:].indirect(lst[:]))
+            d = sb(name + "_sd", [P, S], U8)
+            nc.vector.tensor_copy(
+                d[:].rearrange("p (t a i) -> p a t i", t=PACK, i=16),
+                g[:].rearrange("p (a i t) -> p a t i", t=PACK, i=16),
+            )
+            return d
+
+        def pick_words(name, lst):
+            d = sb(name + "_wd", [P, S], I32)
+            nc.vector.tensor_copy(
+                d[:].bitcast(U32).rearrange("p (t m) -> p m t", t=PACK),
+                xw[:].bitcast(U32).indirect(lst[:]),
+            )
+            return d
+
+        def interleave(copy, dst, src):
+            copy(dst.rearrange("p (c i) t -> p c t i", i=4), src.rearrange("p t (c i) -> p c t i", i=4))
+
+        def quantize(codes, scales, grouped):
+            nc.vector.quantize_mx(out=codes.bitcast(FP8X4), scales=scales, in_=grouped.rearrange("p c t -> p (c t)"))
+
+        def product(bank, lw, ls, t, rw, rs):
+            cols = slice(t * P, (t + 1) * P)
+            nc.tensor.matmul_mx(out=bank[:], lhsT=lw[:, cols].bitcast(FP8X4), lhsT_scale=ls[:, cols],
+                                rhs=rw[:].bitcast(FP8X4), rhs_scale=rs[:], start=True, stop=True)
+
+        two_s = pick_scales("two", two_l)
+        offs_s = pick_scales("offs", offs_l)
+
+        wb_codes = sb("wb_codes", [P, H], U32)
+        wb_scales = sb("wb_scales", [P, H], U8)
+        wb_g = [sb("wb_g%d" % h, [P, HALF, PACK], BF16) for h in range(2)]
+        interleave(nc.scalar.copy, wb_g[0][:], wb_raw[0][:])
+        interleave(nc.scalar.copy, wb_g[1][:], wb_raw[1][:])
+        for h in range(2):
+            cols = slice(h * HALF, (h + 1) * HALF)
+            quantize(wb_codes[:, cols], wb_scales[:, cols], wb_g[h][:])
+
+        two_w = pick_words("two", two_l)
+        b_ps = [psum.tile([P, H], F32, name="b_ps%d" % t, tag="left%d" % t) for t in range(PACK)]
+        b_sb = [sb("b_sb%d" % t, [P, H], F32, "wa_raw0" if t == 0 else None) for t in range(PACK)]
+        for t in range(PACK):
+            product(b_ps[t], two_w, two_s, t, wb_codes, wb_scales)
+
+        offs_w = pick_words("offs", offs_l)
+
+        g1 = [[sb("g1_%d_%d" % (t, h), [P, HALF], F32) for h in range(2)] for t in range(PACK)]
+        dd = [[sb("dd_%d_%d" % (t, h), [P, HALF], F32) for h in range(2)] for t in range(PACK)]
+        th = [[sb("th_%d_%d" % (t, h), [P, HALF], F32) for h in range(2)] for t in range(PACK)]
+        z_rows = [sb("z_rows%d" % h, [P, PACK, HALF], BF16) for h in range(2)]
+        z2_rows = sb("z2_rows", [P, PACK, H], BF16)
+        z_g = sb("z_g", [P, PACK, P, PACK], BF16)
+        z2_g = [sb("z2_g%d" % h, [P, HALF, PACK], BF16, "dd_3_1" if h == 1 else None) for h in range(2)]
+        z_codes = sb("z_codes", [P, H], U32)
+        z_scales = sb("z_scales", [P, H], U8)
+        z2_codes = sb("z2_codes", [P, H], U32)
+        z2_scales = sb("z2_scales", [P, H], U8)
+        wa_codes = sb("wa_codes", [P, H], U32)
+        wa_scales = sb("wa_scales", [P, H], U8)
+        wa_g = [sb("wa_g%d" % h, [P, HALF, PACK], BF16) for h in range(2)]
+        a_ps = [psum.tile([P, H], F32, name="a_ps%d" % t, tag="right%d" % t) for t in range(PACK)]
+
+        def fetch1(t, h):
+            nc.scalar.activation(g1[t][h][:], b_sb[t][:].indirect(half_of(n1_l, h)), ACT.Copy)
+
+        def fetch2(t, h):
+            nc.vector.tensor_tensor(dd[t][h][:], b_sb[t][:].indirect(half_of(n2_l, h)), g1[t][h][:], ALU.subtract)
+
+        def squash(t, h):
+            nc.scalar.activation(th[t][h][:], dd[t][h][:], ACT.Tanh, scale=-1.0)
+
+        def weigh(t, h):
+            nc.vector.scalar_tensor_tensor(z_rows[h][:, t, :], a_ps[t][:, h * HALF : (h + 1) * HALF], gt_t[:, t : t + 1],
+                                           th[t][h][:], ALU.mult, ALU.mult)
+
+        def deal_z(h):
+            nc.vector.tensor_copy(
+                z_g[:, :, h * 64 : (h + 1) * 64, :].rearrange("p u (a i) t -> p a t i u", i=2),
+                z_rows[h][:].rearrange("p t (a i u) -> p a t i u", i=2, u=PACK),
+            )
+
+        interleave(nc.scalar.copy, wa_g[0][:], wa_raw[0][:])
+        interleave(nc.vector.tensor_copy, wa_g[1][:], wa_raw[1][:])
+        for t in range(PACK):
+            nc.scalar.copy(b_sb[t][:], b_ps[t][:])
+            if t < 2:
+                cols = slice(t * HALF, (t + 1) * HALF)
+                quantize(wa_codes[:, cols], wa_scales[:, cols], wa_g[t][:])
+            nc.vector.tensor_scalar(z2_rows[:, t, :], b_sb[t][:], gi_t[:, t : t + 1], None, ALU.mult)
+        for t in range(PACK):
+            product(a_ps[t], offs_w, offs_s, t, wa_codes, wa_scales)
+        for h in range(2):
+            for t in range(PACK):
+                fetch1(t, h)
+                fetch2(t, h)
+        interleave(nc.scalar.copy, z2_g[0][:], z2_rows[:, :, 0:HALF])
+        for h in range(2):
+            for t in range(PACK):
+                squash(t, h)
+                weigh(t, h)
+                if (t, h) == (0, 1):
+                    deal_z(0)
+                if (t, h) == (3, 0):
+                    quantize(z2_codes[:, 0:HALF], z2_scales[:, 0:HALF], z2_g[0][:])
+        interleave(nc.scalar.copy, z2_g[1][:], z2_rows[:, :, HALF:H])
+        deal_z(1)
+        quantize(z2_codes[:, HALF:H], z2_scales[:, HALF:H], z2_g[1][:])
+
+        cv_ps = [psum.tile([P, H], F32, name="cv_ps%d" % u, tag="left%d" % u) for u in range(PACK)]
+        cv = [sb("cv%d" % u, [P, H], F32) for u in range(PACK)]
+        st = [sb("st%d" % u, [P, H], F32) for u in range(PACK)]
+        g3 = [[sb("g3_%d_%d" % (u, h), [P, HALF], F32) for h in range(2)] for u in range(PACK)]
+        g4 = [[sb("g4_%d_%d" % (u, h), [P, HALF], F32) for h in range(2)] for u in range(PACK)]
+        y = [sb("y%d" % h, [P, PACK, HALF], F32) for h in range(2)]
+        y_g = [sb("y_g%d" % h, [P, HALF, PACK], BF16) for h in range(2)]
+        y_codes = sb("y_codes", [P, H], I32)
+        y_scales = sb("y_scales", [P, H], U8)
+        out_rows = out_0.rearrange("(p u) j -> p u j", u=PACK)
+        out_words = out_1[0].rearrange("p c r -> p (c r)").bitcast(I32)
+
+        for u in range(PACK):
+            cols = slice(u * P, (u + 1) * P)
+            quantize(z_codes[:, cols], z_scales[:, cols], z_g[:, u, :, :])
+            product(cv_ps[u], z_codes, z_scales, u, z2_codes, z2_scales)
+
+        def leave(u):
+            if u == 0:
+                nc.scalar.activation(cv[u][:], cv_ps[u][:], ACT.Copy, scale=0.0625)
+            else:
+                nc.vector.tensor_scalar(cv[u][:], cv_ps[u][:], 0.0625, None, ALU.mult)
+
+        def fetch3(u):
+            for h in range(2):
+                nc.scalar.activation(g3[u][h][:], cv[u][:].indirect(half_of(n3_l, h)), ACT.Copy)
+
+        def step(u):
+            for h in range(2):
+                cols = slice(h * HALF, (h + 1) * HALF)
+                nc.vector.tensor_tensor(st[u][:, cols], cv[u][:, cols], g3[u][h][:], ALU.subtract)
+
+        def fetch4(u, h):
+            if u == 0 or (u, h) == (1, 0):
+                nc.vector.tensor_copy(g4[u][h][:], st[u][:].indirect(half_of(n4_l, h)))
+            else:
+                nc.scalar.activation(g4[u][h][:], st[u][:].indirect(half_of(n4_l, h)), ACT.Copy)
+
+        def larger(u, h):
+            cols = slice(h * HALF, (h + 1) * HALF)
+            nc.vector.tensor_tensor(y[h][:, u, :], st[u][:, cols], g4[u][h][:], ALU.max)
+            nc.sync.dma_start(out_rows[:, u, cols], y[h][:, u, :])
+
+        def hand_on(h):
+            cols = slice(h * HALF, (h + 1) * HALF)
+            quantize(y_codes[:, cols], y_scales[:, cols], y_g[h][:])
+            nc.sync.dma_start(out_words[:, cols], y_codes[:, cols])
+
+        for u in range(PACK):
+            leave(u)
+        for u in range(PACK):
+            fetch3(u)
+            step(u)
+            if u < 2:
+                fetch4(0, u)
+            if u == 1:
+                larger(0, 0)
+        larger(0, 1)
+        fetch4(1, 0)
+        for u, h in ((1, 1), (2, 0), (1, 0), (3, 0), (2, 1), (3, 1)):
+            if (u, h) != (1, 0):
+                fetch4(u, h)
+            larger(u, h)
+        interleave(nc.scalar.copy, y_g[0][:], y[0][:])
+        interleave(nc.vector.tensor_copy, y_g[1][:], y[1][:])
+        for h in range(2):
+            hand_on(h)
+        for q in range(4):
+            eng = nc.scalar if q % 2 else nc.sync
+            eng.dma_start(out_2[0, 4 * q : 4 * q + 4, :].bitcast(I32), y_scales[32 * q : 32 * q + 4, :].bitcast(I32))

@@ -1,6 +1,7 @@
 from contextlib import ExitStack
 
 import concourse.mybir as mybir
+from concourse.masks import make_identity
 
 K, T, S, H = 512, 2048, 512, 512
 FLOPS = 3 * 2 * 512 * 512 * 512
@@ -40,29 +41,32 @@ def tile_picked_momtjointbhopmx_none_po_kernel(tc, x_words, x_scales, wa, wb, gt
 
         xs = sb("xs", [P, T], U8)
         nc.vector.memset(xs[:].bitcast(I32), 0)
+        gates_in = sb("gates_in", [P, P], F32)
+        nc.gpsimd.memset(gates_in[:], 0.0)
+        ident = sb("ident", [P, P], F32)
+        make_identity(nc, ident[:])
         two_l = load_list("two_l", two)
         offs_l = load_list("offs_l", offs)
+        def load_half(dst, w, h):
+            nc.sync.dma_start(dst[:], w.rearrange("(p j) c -> p j c", j=PACK)[:, :, h * HALF : (h + 1) * HALF])
+
+        wb_raw = [sb("wb_raw%d" % h, [P, PACK, HALF], F32) for h in range(2)]
+        wa_raw = [sb("wa_raw%d" % h, [P, PACK, HALF], F32) for h in range(2)]
+        load_half(wb_raw[0], wb, 0)
         for q in range(4):
             nc.sync.dma_start(xs[32 * q : 32 * q + 4, :].bitcast(I32), x_scales[0, 4 * q : 4 * q + 4, :].bitcast(I32))
-
-        def load_w(name, w):
-            halves = []
-            for h in range(2):
-                t = sb("%s_raw%d" % (name, h), [P, PACK, HALF], F32)
-                nc.sync.dma_start(t[:], w.rearrange("(p j) c -> p j c", j=PACK)[:, :, h * HALF : (h + 1) * HALF])
-                halves.append(t)
-            return halves
-
-        wb_raw = load_w("wb", wb)
+        load_half(wb_raw[1], wb, 1)
         xw = sb("xw", [P, T], I32)
         nc.sync.dma_start(xw[:], x_words[0].rearrange("p c r -> p (c r)").bitcast(I32))
-        wa_raw = load_w("wa", wa)
-        gi_t = sb("gi_t", [P, PACK], F32)
-        nc.sync.dma_start(gi_t[:], gi.rearrange("(p t) o -> p (t o)", t=PACK))
+        for h in range(2):
+            load_half(wa_raw[h], wa, h)
+        for k, g in enumerate((gt, gi)):
+            nc.sync.dma_start(
+                gates_in[PACK * k : PACK * (k + 1), :].rearrange("t (b r) -> t b r", r=8),
+                g.rearrange("(b t r) o -> t b (r o)", t=PACK, r=8),
+            )
         n1_l = load_list("n1_l", n1)
         n2_l = load_list("n2_l", n2)
-        gt_t = sb("gt_t", [P, PACK], F32)
-        nc.sync.dma_start(gt_t[:], gt.rearrange("(p t) o -> p (t o)", t=PACK))
         n3_l = load_list("n3_l", n3)
         n4_l = load_list("n4_l", n4)
 
@@ -71,15 +75,15 @@ def tile_picked_momtjointbhopmx_none_po_kernel(tc, x_words, x_scales, wa, wb, gt
             nc.vector.tensor_copy(g[:], xs[:].indirect(lst[:]))
             d = sb(name + "_sd", [P, S], U8)
             nc.vector.tensor_copy(
-                d[:].rearrange("p (t a i) -> p a t i", t=PACK, i=16),
-                g[:].rearrange("p (a i t) -> p a t i", t=PACK, i=16),
+                d[:].bitcast(I32).rearrange("p (t a b w) -> p a t b w", t=PACK, b=2, w=2),
+                g[:].bitcast(I32).rearrange("p (a b t w) -> p a t b w", t=PACK, b=2, w=2),
             )
             return d
 
         def pick_words(name, lst):
             d = sb(name + "_wd", [P, S], I32)
             nc.vector.tensor_copy(
-                d[:].bitcast(U32).rearrange("p (t m) -> p m t", t=PACK),
+                d[:].bitcast(U32).rearrange("p (t b r) -> p b t r", t=PACK, r=8),
                 xw[:].bitcast(U32).indirect(lst[:]),
             )
             return d
@@ -90,16 +94,16 @@ def tile_picked_momtjointbhopmx_none_po_kernel(tc, x_words, x_scales, wa, wb, gt
         def quantize(codes, scales, grouped):
             nc.vector.quantize_mx(out=codes.bitcast(FP8X4), scales=scales, in_=grouped.rearrange("p c t -> p (c t)"))
 
-        def product(bank, lw, ls, t, rw, rs):
+        def product(bank, lw, ls, t, rw, rs, moving=slice(0, H)):
             cols = slice(t * P, (t + 1) * P)
             nc.tensor.matmul_mx(out=bank[:], lhsT=lw[:, cols].bitcast(FP8X4), lhsT_scale=ls[:, cols],
-                                rhs=rw[:].bitcast(FP8X4), rhs_scale=rs[:], start=True, stop=True)
+                                rhs=rw[:, moving].bitcast(FP8X4), rhs_scale=rs[:, moving], start=True, stop=True)
 
         two_s = pick_scales("two", two_l)
         offs_s = pick_scales("offs", offs_l)
 
         wb_codes = sb("wb_codes", [P, H], U32)
-        wb_scales = sb("wb_scales", [P, H], U8)
+        wb_scales = sb("wb_scales", [P, H], U8, "two_sg")
         wb_g = [sb("wb_g%d" % h, [P, HALF, PACK], BF16) for h in range(2)]
         interleave(nc.scalar.copy, wb_g[0][:], wb_raw[0][:])
         interleave(nc.scalar.copy, wb_g[1][:], wb_raw[1][:])
@@ -108,20 +112,32 @@ def tile_picked_momtjointbhopmx_none_po_kernel(tc, x_words, x_scales, wa, wb, gt
             quantize(wb_codes[:, cols], wb_scales[:, cols], wb_g[h][:])
 
         two_w = pick_words("two", two_l)
-        b_ps = [psum.tile([P, H], F32, name="b_ps%d" % t, tag="left%d" % t) for t in range(PACK)]
-        b_sb = [sb("b_sb%d" % t, [P, H], F32, "wa_raw0" if t == 0 else None) for t in range(PACK)]
-        for t in range(PACK):
+        b0_ps = [psum.tile([P, HALF], F32, name="b0_ps%d" % h, tag=("left0", "right0")[h]) for h in range(2)]
+        b_ps = [None] + [psum.tile([P, H], F32, name="b_ps%d" % t, tag="left%d" % t) for t in range(1, PACK)]
+        b_sb = [sb("b_sb0", [P, H], F32, "wa_raw0")] + [sb("b_sb%d" % t, [P, 2 * H], F32) for t in range(1, PACK)]
+        cv = [sb("cv%d" % u, [P, H + 8], F32) for u in range(PACK)]
+        for t in range(1, PACK):
+            nc.vector.memset(b_sb[t][:, H:], 0.0)
+        for u in range(PACK):
+            nc.vector.memset(cv[u][:, H:], 0.0)
+        for h in range(2):
+            product(b0_ps[h], two_w, two_s, 0, wb_codes, wb_scales, slice(h * HALF, (h + 1) * HALF))
+        for t in range(1, PACK):
             product(b_ps[t], two_w, two_s, t, wb_codes, wb_scales)
 
+        gates_ps = psum.tile([P, P], F32, name="gates_ps", tag="right1")
+        nc.tensor.transpose(gates_ps[:], gates_in[:], ident[:])
+        gates = sb("gates", [P, 2 * PACK], F32)
+        nc.scalar.copy(gates[:], gates_ps[:, 0 : 2 * PACK])
         offs_w = pick_words("offs", offs_l)
 
-        g1 = [[sb("g1_%d_%d" % (t, h), [P, HALF], F32) for h in range(2)] for t in range(PACK)]
-        dd = [[sb("dd_%d_%d" % (t, h), [P, HALF], F32) for h in range(2)] for t in range(PACK)]
+        g1 = [sb("g1_%d" % t, [P, H], F32) for t in range(PACK)]
+        dd = [sb("dd_%d" % t, [P, H], F32) for t in range(PACK)]
         th = [[sb("th_%d_%d" % (t, h), [P, HALF], F32) for h in range(2)] for t in range(PACK)]
         z_rows = [sb("z_rows%d" % h, [P, PACK, HALF], BF16) for h in range(2)]
         z2_rows = sb("z2_rows", [P, PACK, H], BF16)
         z_g = sb("z_g", [P, PACK, P, PACK], BF16)
-        z2_g = [sb("z2_g%d" % h, [P, HALF, PACK], BF16, "dd_3_1" if h == 1 else None) for h in range(2)]
+        z2_g = [sb("z2_g%d" % h, [P, HALF, PACK], BF16, "dd_%d" % (2 + h)) for h in range(2)]
         z_codes = sb("z_codes", [P, H], U32)
         z_scales = sb("z_scales", [P, H], U8)
         z2_codes = sb("z2_codes", [P, H], U32)
@@ -131,56 +147,64 @@ def tile_picked_momtjointbhopmx_none_po_kernel(tc, x_words, x_scales, wa, wb, gt
         wa_g = [sb("wa_g%d" % h, [P, HALF, PACK], BF16) for h in range(2)]
         a_ps = [psum.tile([P, H], F32, name="a_ps%d" % t, tag="right%d" % t) for t in range(PACK)]
 
-        def fetch1(t, h):
-            nc.scalar.activation(g1[t][h][:], b_sb[t][:].indirect(half_of(n1_l, h)), ACT.Copy)
-
-        def fetch2(t, h):
-            nc.vector.tensor_tensor(dd[t][h][:], b_sb[t][:].indirect(half_of(n2_l, h)), g1[t][h][:], ALU.subtract)
+        def fetch12(t, first, last):
+            cols = slice(first, last)
+            entries = slice(first // 16, last // 16)
+            nc.scalar.activation(g1[t][:, cols], b_sb[t][:].indirect(n1_l[:, entries]), ACT.Copy)
+            nc.vector.tensor_tensor(dd[t][:, cols], b_sb[t][:].indirect(n2_l[:, entries]), g1[t][:, cols], ALU.subtract)
 
         def squash(t, h):
-            nc.scalar.activation(th[t][h][:], dd[t][h][:], ACT.Tanh, scale=-1.0)
+            nc.scalar.activation(th[t][h][:], dd[t][:, h * HALF : (h + 1) * HALF], ACT.Tanh, scale=-1.0)
 
         def weigh(t, h):
-            nc.vector.scalar_tensor_tensor(z_rows[h][:, t, :], a_ps[t][:, h * HALF : (h + 1) * HALF], gt_t[:, t : t + 1],
+            nc.vector.scalar_tensor_tensor(z_rows[h][:, t, :], a_ps[t][:, h * HALF : (h + 1) * HALF], gates[:, t : t + 1],
                                            th[t][h][:], ALU.mult, ALU.mult)
 
-        def deal_z(h):
+        def deal_z(h, first=0, last=PACK):
             nc.vector.tensor_copy(
-                z_g[:, :, h * 64 : (h + 1) * 64, :].rearrange("p u (a i) t -> p a t i u", i=2),
-                z_rows[h][:].rearrange("p t (a i u) -> p a t i u", i=2, u=PACK),
+                z_g[:, first:last, h * 64 : (h + 1) * 64, :].rearrange("p u (a i) t -> p a t i u", i=2),
+                z_rows[h][:].rearrange("p t (a i u) -> p a t i u", i=2, u=PACK)[:, :, :, :, first:last],
             )
 
         interleave(nc.scalar.copy, wa_g[0][:], wa_raw[0][:])
         interleave(nc.vector.tensor_copy, wa_g[1][:], wa_raw[1][:])
         for t in range(PACK):
-            nc.scalar.copy(b_sb[t][:], b_ps[t][:])
+            if t == 0:
+                for h in range(2):
+                    nc.scalar.copy(b_sb[0][:, h * HALF : (h + 1) * HALF], b0_ps[h][:])
+            elif t == 2:
+                nc.scalar.copy(b_sb[t][:, 0:H], b_ps[t][:])
+            else:
+                nc.vector.tensor_copy(b_sb[t][:, 0:H], b_ps[t][:])
             if t < 2:
                 cols = slice(t * HALF, (t + 1) * HALF)
                 quantize(wa_codes[:, cols], wa_scales[:, cols], wa_g[t][:])
-            nc.vector.tensor_scalar(z2_rows[:, t, :], b_sb[t][:], gi_t[:, t : t + 1], None, ALU.mult)
+        for t in range(PACK):
+            nc.vector.tensor_scalar(z2_rows[:, t, :], b_sb[t][:, 0:H], gates[:, PACK + t : PACK + t + 1], None, ALU.mult)
         for t in range(PACK):
             product(a_ps[t], offs_w, offs_s, t, wa_codes, wa_scales)
-        for h in range(2):
-            for t in range(PACK):
-                fetch1(t, h)
-                fetch2(t, h)
-        interleave(nc.scalar.copy, z2_g[0][:], z2_rows[:, :, 0:HALF])
+        fetch12(0, 0, HALF)
+        fetch12(0, HALF, H)
+        for t in range(1, PACK):
+            fetch12(t, 0, H)
         for h in range(2):
             for t in range(PACK):
                 squash(t, h)
+        for h in range(2):
+            interleave(nc.scalar.copy, z2_g[h][:], z2_rows[:, :, h * HALF : (h + 1) * HALF])
+        for h in range(2):
+            for t in range(PACK):
                 weigh(t, h)
                 if (t, h) == (0, 1):
                     deal_z(0)
-                if (t, h) == (3, 0):
-                    quantize(z2_codes[:, 0:HALF], z2_scales[:, 0:HALF], z2_g[0][:])
-        interleave(nc.scalar.copy, z2_g[1][:], z2_rows[:, :, HALF:H])
-        deal_z(1)
+        quantize(z2_codes[:, 0:HALF], z2_scales[:, 0:HALF], z2_g[0][:])
+        deal_z(1, 0, 1)
         quantize(z2_codes[:, HALF:H], z2_scales[:, HALF:H], z2_g[1][:])
 
-        cv_ps = [psum.tile([P, H], F32, name="cv_ps%d" % u, tag="left%d" % u) for u in range(PACK)]
-        cv = [sb("cv%d" % u, [P, H], F32) for u in range(PACK)]
+        cv0_ps = [psum.tile([P, HALF], F32, name="cv0_ps%d" % h, tag="left%d" % h) for h in range(2)]
+        cv_ps = [None] + [psum.tile([P, H], F32, name="cv_ps%d" % u, tag=("left2", "left3", "right0")[u - 1]) for u in range(1, PACK)]
         st = [sb("st%d" % u, [P, H], F32) for u in range(PACK)]
-        g3 = [[sb("g3_%d_%d" % (u, h), [P, HALF], F32) for h in range(2)] for u in range(PACK)]
+        g3 = [sb("g3_%d" % u, [P, H], F32) for u in range(PACK)]
         g4 = [[sb("g4_%d_%d" % (u, h), [P, HALF], F32) for h in range(2)] for u in range(PACK)]
         y = [sb("y%d" % h, [P, PACK, HALF], F32) for h in range(2)]
         y_g = [sb("y_g%d" % h, [P, HALF, PACK], BF16) for h in range(2)]
@@ -192,22 +216,25 @@ def tile_picked_momtjointbhopmx_none_po_kernel(tc, x_words, x_scales, wa, wb, gt
         for u in range(PACK):
             cols = slice(u * P, (u + 1) * P)
             quantize(z_codes[:, cols], z_scales[:, cols], z_g[:, u, :, :])
-            product(cv_ps[u], z_codes, z_scales, u, z2_codes, z2_scales)
+            if u == 0:
+                deal_z(1, 1, PACK)
+                for h in range(2):
+                    product(cv0_ps[h], z_codes, z_scales, 0, z2_codes, z2_scales, slice(h * HALF, (h + 1) * HALF))
+            else:
+                product(cv_ps[u], z_codes, z_scales, u, z2_codes, z2_scales)
 
         def leave(u):
             if u == 0:
-                nc.scalar.activation(cv[u][:], cv_ps[u][:], ACT.Copy, scale=0.0625)
+                nc.scalar.activation(cv[0][:, 0:HALF], cv0_ps[0][:], ACT.Copy, scale=0.0625)
+                nc.vector.tensor_scalar(cv[0][:, HALF:H], cv0_ps[1][:], 0.0625, None, ALU.mult)
             else:
-                nc.vector.tensor_scalar(cv[u][:], cv_ps[u][:], 0.0625, None, ALU.mult)
+                nc.vector.tensor_scalar(cv[u][:, 0:H], cv_ps[u][:], 0.0625, None, ALU.mult)
 
         def fetch3(u):
-            for h in range(2):
-                nc.scalar.activation(g3[u][h][:], cv[u][:].indirect(half_of(n3_l, h)), ACT.Copy)
+            nc.scalar.activation(g3[u][:], cv[u][:].indirect(n3_l[:]), ACT.Copy)
 
         def step(u):
-            for h in range(2):
-                cols = slice(h * HALF, (h + 1) * HALF)
-                nc.vector.tensor_tensor(st[u][:, cols], cv[u][:, cols], g3[u][h][:], ALU.subtract)
+            nc.vector.tensor_tensor(st[u][:], cv[u][:, 0:H], g3[u][:], ALU.subtract)
 
         def fetch4(u, h):
             if u == 0 or (u, h) == (1, 0):
@@ -230,16 +257,14 @@ def tile_picked_momtjointbhopmx_none_po_kernel(tc, x_words, x_scales, wa, wb, gt
         for u in range(PACK):
             fetch3(u)
             step(u)
-            if u < 2:
-                fetch4(0, u)
-            if u == 1:
-                larger(0, 0)
-        larger(0, 1)
-        fetch4(1, 0)
-        for u, h in ((1, 1), (2, 0), (1, 0), (3, 0), (2, 1), (3, 1)):
-            if (u, h) != (1, 0):
-                fetch4(u, h)
-            larger(u, h)
+            if u in (1, 2):
+                fetch4(u - 1, 0)
+        fetch4(0, 1)
+        for u, h in ((2, 0), (3, 0), (1, 1), (2, 1), (3, 1)):
+            fetch4(u, h)
+        for h in range(2):
+            for u in range(PACK):
+                larger(u, h)
         interleave(nc.scalar.copy, y_g[0][:], y[0][:])
         interleave(nc.vector.tensor_copy, y_g[1][:], y[1][:])
         for h in range(2):

@@ -3,7 +3,7 @@ from contextlib import ExitStack
 import concourse.mybir as mybir
 from concourse.masks import make_identity
 
-K, T, S, H = 512, 2048, 512, 512
+T, S, H = 2048, 512, 512
 FLOPS = 3 * 2 * 512 * 512 * 512
 
 F32 = mybir.dt.float32
@@ -18,26 +18,39 @@ ACT = mybir.ActivationFunctionType
 
 P = 128
 PACK = 4
+RUN = 8
+LANES = 16
+QUADRANT = 32
 HALF = H // 2
-HALF_COLS = HALF // 16
+SPARE = 8
+CV_SCALE = 0.0625
+N4_ON_VECTOR = ((0, 0), (1, 0), (0, 1))
 
 
-def tile_picked_momtjointbhopmx_none_po_kernel(tc, x_words, x_scales, wa, wb, gt, gi, offs, two, n1, n2, n3, n4, out_0, out_1, out_2):
+def tile_picked_momtjointbhopmx_none_po_kernel(
+    tc, x_words, x_scales, wa, wb, gt, gi, offs, two, n1, n2, n3, n4, out_0, out_1, out_2
+):
     nc = tc.nc
     with ExitStack() as ctx:
         keep = ctx.enter_context(tc.tile_pool(name="keep", bufs=1))
         psum = ctx.enter_context(tc.psum_pool(name="psum", bufs=1))
 
-        def sb(name, shape, dtype, tag=None):
-            return keep.tile(shape, dtype, name=name, tag=tag or name, align_bytes=64)
+        def sb(name, shape, dtype, reuses=None):
+            return keep.tile(shape, dtype, name=name, tag=reuses or name, align_bytes=64)
+
+        def half(h):
+            return slice(h * HALF, (h + 1) * HALF)
 
         def load_list(name, src):
-            t = sb(name, [P, 32], U16)
-            nc.sync.dma_start(t[:], src)
-            return t
+            lst = sb(name, [P, S // LANES], U16)
+            nc.sync.dma_start(lst[:], src)
+            return lst
 
-        def half_of(lst, h):
-            return lst[:, h * HALF_COLS : (h + 1) * HALF_COLS]
+        def entries(lst, cols):
+            return lst[:, cols.start // LANES : cols.stop // LANES]
+
+        def load_weight_half(dst, w, h):
+            nc.sync.dma_start(dst[:], w.rearrange("(p j) c -> p j c", j=PACK)[:, :, half(h)])
 
         xs = sb("xs", [P, T], U8)
         nc.vector.memset(xs[:].bitcast(I32), 0)
@@ -47,23 +60,22 @@ def tile_picked_momtjointbhopmx_none_po_kernel(tc, x_words, x_scales, wa, wb, gt
         make_identity(nc, ident[:])
         two_l = load_list("two_l", two)
         offs_l = load_list("offs_l", offs)
-        def load_half(dst, w, h):
-            nc.sync.dma_start(dst[:], w.rearrange("(p j) c -> p j c", j=PACK)[:, :, h * HALF : (h + 1) * HALF])
-
         wb_raw = [sb("wb_raw%d" % h, [P, PACK, HALF], F32) for h in range(2)]
         wa_raw = [sb("wa_raw%d" % h, [P, PACK, HALF], F32) for h in range(2)]
-        load_half(wb_raw[0], wb, 0)
-        for q in range(4):
-            nc.sync.dma_start(xs[32 * q : 32 * q + 4, :].bitcast(I32), x_scales[0, 4 * q : 4 * q + 4, :].bitcast(I32))
-        load_half(wb_raw[1], wb, 1)
+        load_weight_half(wb_raw[0], wb, 0)
+        for q in range(P // QUADRANT):
+            nc.sync.dma_start(
+                xs[QUADRANT * q : QUADRANT * q + 4, :].bitcast(I32), x_scales[0, 4 * q : 4 * q + 4, :].bitcast(I32)
+            )
+        load_weight_half(wb_raw[1], wb, 1)
         xw = sb("xw", [P, T], I32)
         nc.sync.dma_start(xw[:], x_words[0].rearrange("p c r -> p (c r)").bitcast(I32))
         for h in range(2):
-            load_half(wa_raw[h], wa, h)
-        for k, g in enumerate((gt, gi)):
+            load_weight_half(wa_raw[h], wa, h)
+        for first_row, gate in ((0, gt), (PACK, gi)):
             nc.sync.dma_start(
-                gates_in[PACK * k : PACK * (k + 1), :].rearrange("t (b r) -> t b r", r=8),
-                g.rearrange("(b t r) o -> t b (r o)", t=PACK, r=8),
+                gates_in[first_row : first_row + PACK, :].rearrange("t (b r) -> t b r", r=RUN),
+                gate.rearrange("(b t r) o -> t b (r o)", t=PACK, r=RUN),
             )
         n1_l = load_list("n1_l", n1)
         n2_l = load_list("n2_l", n2)
@@ -71,22 +83,22 @@ def tile_picked_momtjointbhopmx_none_po_kernel(tc, x_words, x_scales, wa, wb, gt
         n4_l = load_list("n4_l", n4)
 
         def pick_scales(name, lst):
-            g = sb(name + "_sg", [P, S], U8)
-            nc.vector.tensor_copy(g[:], xs[:].indirect(lst[:]))
-            d = sb(name + "_sd", [P, S], U8)
+            gathered = sb(name + "_sg", [P, S], U8)
+            nc.vector.tensor_copy(gathered[:], xs[:].indirect(lst[:]))
+            dealt = sb(name + "_sd", [P, S], U8)
             nc.vector.tensor_copy(
-                d[:].bitcast(I32).rearrange("p (t a b w) -> p a t b w", t=PACK, b=2, w=2),
-                g[:].bitcast(I32).rearrange("p (a b t w) -> p a t b w", t=PACK, b=2, w=2),
+                dealt[:].bitcast(I32).rearrange("p (t a b w) -> p a t b w", t=PACK, b=2, w=2),
+                gathered[:].bitcast(I32).rearrange("p (a b t w) -> p a t b w", t=PACK, b=2, w=2),
             )
-            return d
+            return dealt
 
         def pick_words(name, lst):
-            d = sb(name + "_wd", [P, S], I32)
+            dealt = sb(name + "_wd", [P, S], I32)
             nc.vector.tensor_copy(
-                d[:].bitcast(U32).rearrange("p (t b r) -> p b t r", t=PACK, r=8),
+                dealt[:].bitcast(U32).rearrange("p (t b r) -> p b t r", t=PACK, r=RUN),
                 xw[:].bitcast(U32).indirect(lst[:]),
             )
-            return d
+            return dealt
 
         def interleave(copy, dst, src):
             copy(dst.rearrange("p (c i) t -> p c t i", i=4), src.rearrange("p t (c i) -> p c t i", i=4))
@@ -94,10 +106,17 @@ def tile_picked_momtjointbhopmx_none_po_kernel(tc, x_words, x_scales, wa, wb, gt
         def quantize(codes, scales, grouped):
             nc.vector.quantize_mx(out=codes.bitcast(FP8X4), scales=scales, in_=grouped.rearrange("p c t -> p (c t)"))
 
-        def product(bank, lw, ls, t, rw, rs, moving=slice(0, H)):
-            cols = slice(t * P, (t + 1) * P)
-            nc.tensor.matmul_mx(out=bank[:], lhsT=lw[:, cols].bitcast(FP8X4), lhsT_scale=ls[:, cols],
-                                rhs=rw[:, moving].bitcast(FP8X4), rhs_scale=rs[:, moving], start=True, stop=True)
+        def product(bank, l_codes, l_scales, tile_no, r_codes, r_scales, moving=slice(0, H)):
+            rows = slice(tile_no * P, (tile_no + 1) * P)
+            nc.tensor.matmul_mx(
+                out=bank[:],
+                lhsT=l_codes[:, rows].bitcast(FP8X4),
+                lhsT_scale=l_scales[:, rows],
+                rhs=r_codes[:, moving].bitcast(FP8X4),
+                rhs_scale=r_scales[:, moving],
+                start=True,
+                stop=True,
+            )
 
         two_s = pick_scales("two", two_l)
         offs_s = pick_scales("offs", offs_l)
@@ -105,23 +124,22 @@ def tile_picked_momtjointbhopmx_none_po_kernel(tc, x_words, x_scales, wa, wb, gt
         wb_codes = sb("wb_codes", [P, H], U32)
         wb_scales = sb("wb_scales", [P, H], U8, "two_sg")
         wb_g = [sb("wb_g%d" % h, [P, HALF, PACK], BF16) for h in range(2)]
-        interleave(nc.scalar.copy, wb_g[0][:], wb_raw[0][:])
-        interleave(nc.scalar.copy, wb_g[1][:], wb_raw[1][:])
         for h in range(2):
-            cols = slice(h * HALF, (h + 1) * HALF)
-            quantize(wb_codes[:, cols], wb_scales[:, cols], wb_g[h][:])
+            interleave(nc.scalar.copy, wb_g[h][:], wb_raw[h][:])
+        for h in range(2):
+            quantize(wb_codes[:, half(h)], wb_scales[:, half(h)], wb_g[h][:])
 
         two_w = pick_words("two", two_l)
         b0_ps = [psum.tile([P, HALF], F32, name="b0_ps%d" % h, tag=("left0", "right0")[h]) for h in range(2)]
-        b_ps = [None] + [psum.tile([P, H], F32, name="b_ps%d" % t, tag="left%d" % t) for t in range(1, PACK)]
+        b_ps = {t: psum.tile([P, H], F32, name="b_ps%d" % t, tag="left%d" % t) for t in range(1, PACK)}
         b_sb = [sb("b_sb0", [P, H], F32, "wa_raw0")] + [sb("b_sb%d" % t, [P, 2 * H], F32) for t in range(1, PACK)]
-        cv = [sb("cv%d" % u, [P, H + 8], F32) for u in range(PACK)]
+        cv = [sb("cv%d" % u, [P, H + SPARE], F32) for u in range(PACK)]
         for t in range(1, PACK):
             nc.vector.memset(b_sb[t][:, H:], 0.0)
         for u in range(PACK):
             nc.vector.memset(cv[u][:, H:], 0.0)
         for h in range(2):
-            product(b0_ps[h], two_w, two_s, 0, wb_codes, wb_scales, slice(h * HALF, (h + 1) * HALF))
+            product(b0_ps[h], two_w, two_s, 0, wb_codes, wb_scales, half(h))
         for t in range(1, PACK):
             product(b_ps[t], two_w, two_s, t, wb_codes, wb_scales)
 
@@ -131,8 +149,8 @@ def tile_picked_momtjointbhopmx_none_po_kernel(tc, x_words, x_scales, wa, wb, gt
         nc.scalar.copy(gates[:], gates_ps[:, 0 : 2 * PACK])
         offs_w = pick_words("offs", offs_l)
 
-        g1 = [sb("g1_%d" % t, [P, H], F32) for t in range(PACK)]
-        dd = [sb("dd_%d" % t, [P, H], F32) for t in range(PACK)]
+        b_n1 = [sb("g1_%d" % t, [P, H], F32) for t in range(PACK)]
+        diff = [sb("dd_%d" % t, [P, H], F32) for t in range(PACK)]
         th = [[sb("th_%d_%d" % (t, h), [P, HALF], F32) for h in range(2)] for t in range(PACK)]
         z_rows = [sb("z_rows%d" % h, [P, PACK, HALF], BF16) for h in range(2)]
         z2_rows = sb("z2_rows", [P, PACK, H], BF16)
@@ -147,65 +165,59 @@ def tile_picked_momtjointbhopmx_none_po_kernel(tc, x_words, x_scales, wa, wb, gt
         wa_g = [sb("wa_g%d" % h, [P, HALF, PACK], BF16) for h in range(2)]
         a_ps = [psum.tile([P, H], F32, name="a_ps%d" % t, tag="right%d" % t) for t in range(PACK)]
 
-        def fetch12(t, first, last):
-            cols = slice(first, last)
-            entries = slice(first // 16, last // 16)
-            nc.scalar.activation(g1[t][:, cols], b_sb[t][:].indirect(n1_l[:, entries]), ACT.Copy)
-            nc.vector.tensor_tensor(dd[t][:, cols], b_sb[t][:].indirect(n2_l[:, entries]), g1[t][:, cols], ALU.subtract)
+        def difference(t, cols):
+            nc.scalar.activation(b_n1[t][:, cols], b_sb[t][:].indirect(entries(n1_l, cols)), ACT.Copy)
+            nc.vector.tensor_tensor(
+                diff[t][:, cols], b_sb[t][:].indirect(entries(n2_l, cols)), b_n1[t][:, cols], ALU.subtract
+            )
 
-        def squash(t, h):
-            nc.scalar.activation(th[t][h][:], dd[t][:, h * HALF : (h + 1) * HALF], ACT.Tanh, scale=-1.0)
-
-        def weigh(t, h):
-            nc.vector.scalar_tensor_tensor(z_rows[h][:, t, :], a_ps[t][:, h * HALF : (h + 1) * HALF], gates[:, t : t + 1],
-                                           th[t][h][:], ALU.mult, ALU.mult)
-
-        def deal_z(h, first=0, last=PACK):
+        def deal_z(h, first, last):
             nc.vector.tensor_copy(
-                z_g[:, first:last, h * 64 : (h + 1) * 64, :].rearrange("p u (a i) t -> p a t i u", i=2),
-                z_rows[h][:].rearrange("p t (a i u) -> p a t i u", i=2, u=PACK)[:, :, :, :, first:last],
+                z_g[:, first:last, h * (P // 2) : (h + 1) * (P // 2), :].rearrange("p u (c i) t -> p c t i u", i=2),
+                z_rows[h][:].rearrange("p t (c i u) -> p c t i u", i=2, u=PACK)[:, :, :, :, first:last],
             )
 
         interleave(nc.scalar.copy, wa_g[0][:], wa_raw[0][:])
         interleave(nc.vector.tensor_copy, wa_g[1][:], wa_raw[1][:])
+        for h in range(2):
+            nc.scalar.copy(b_sb[0][:, half(h)], b0_ps[h][:])
+        quantize(wa_codes[:, half(0)], wa_scales[:, half(0)], wa_g[0][:])
+        nc.vector.tensor_copy(b_sb[1][:, 0:H], b_ps[1][:])
+        quantize(wa_codes[:, half(1)], wa_scales[:, half(1)], wa_g[1][:])
+        nc.scalar.copy(b_sb[2][:, 0:H], b_ps[2][:])
+        nc.vector.tensor_copy(b_sb[3][:, 0:H], b_ps[3][:])
         for t in range(PACK):
-            if t == 0:
-                for h in range(2):
-                    nc.scalar.copy(b_sb[0][:, h * HALF : (h + 1) * HALF], b0_ps[h][:])
-            elif t == 2:
-                nc.scalar.copy(b_sb[t][:, 0:H], b_ps[t][:])
-            else:
-                nc.vector.tensor_copy(b_sb[t][:, 0:H], b_ps[t][:])
-            if t < 2:
-                cols = slice(t * HALF, (t + 1) * HALF)
-                quantize(wa_codes[:, cols], wa_scales[:, cols], wa_g[t][:])
-        for t in range(PACK):
-            nc.vector.tensor_scalar(z2_rows[:, t, :], b_sb[t][:, 0:H], gates[:, PACK + t : PACK + t + 1], None, ALU.mult)
+            nc.vector.tensor_scalar(
+                z2_rows[:, t, :], b_sb[t][:, 0:H], gates[:, PACK + t : PACK + t + 1], None, ALU.mult
+            )
         for t in range(PACK):
             product(a_ps[t], offs_w, offs_s, t, wa_codes, wa_scales)
-        fetch12(0, 0, HALF)
-        fetch12(0, HALF, H)
+        for h in range(2):
+            difference(0, half(h))
         for t in range(1, PACK):
-            fetch12(t, 0, H)
+            difference(t, slice(0, H))
         for h in range(2):
             for t in range(PACK):
-                squash(t, h)
+                nc.scalar.activation(th[t][h][:], diff[t][:, half(h)], ACT.Tanh, scale=-1.0)
         for h in range(2):
-            interleave(nc.scalar.copy, z2_g[h][:], z2_rows[:, :, h * HALF : (h + 1) * HALF])
+            interleave(nc.scalar.copy, z2_g[h][:], z2_rows[:, :, half(h)])
         for h in range(2):
             for t in range(PACK):
-                weigh(t, h)
+                nc.vector.scalar_tensor_tensor(
+                    z_rows[h][:, t, :], a_ps[t][:, half(h)], gates[:, t : t + 1], th[t][h][:], ALU.mult, ALU.mult
+                )
                 if (t, h) == (0, 1):
-                    deal_z(0)
-        quantize(z2_codes[:, 0:HALF], z2_scales[:, 0:HALF], z2_g[0][:])
+                    deal_z(0, 0, PACK)
+        quantize(z2_codes[:, half(0)], z2_scales[:, half(0)], z2_g[0][:])
         deal_z(1, 0, 1)
-        quantize(z2_codes[:, HALF:H], z2_scales[:, HALF:H], z2_g[1][:])
+        quantize(z2_codes[:, half(1)], z2_scales[:, half(1)], z2_g[1][:])
 
         cv0_ps = [psum.tile([P, HALF], F32, name="cv0_ps%d" % h, tag="left%d" % h) for h in range(2)]
-        cv_ps = [None] + [psum.tile([P, H], F32, name="cv_ps%d" % u, tag=("left2", "left3", "right0")[u - 1]) for u in range(1, PACK)]
+        cv_banks = {1: "left2", 2: "left3", 3: "right0"}
+        cv_ps = {u: psum.tile([P, H], F32, name="cv_ps%d" % u, tag=cv_banks[u]) for u in range(1, PACK)}
         st = [sb("st%d" % u, [P, H], F32) for u in range(PACK)]
-        g3 = [sb("g3_%d" % u, [P, H], F32) for u in range(PACK)]
-        g4 = [[sb("g4_%d_%d" % (u, h), [P, HALF], F32) for h in range(2)] for u in range(PACK)]
+        cv_n3 = [sb("g3_%d" % u, [P, H], F32) for u in range(PACK)]
+        st_n4 = [[sb("g4_%d_%d" % (u, h), [P, HALF], F32) for h in range(2)] for u in range(PACK)]
         y = [sb("y%d" % h, [P, PACK, HALF], F32) for h in range(2)]
         y_g = [sb("y_g%d" % h, [P, HALF, PACK], BF16) for h in range(2)]
         y_codes = sb("y_codes", [P, H], I32)
@@ -213,62 +225,52 @@ def tile_picked_momtjointbhopmx_none_po_kernel(tc, x_words, x_scales, wa, wb, gt
         out_rows = out_0.rearrange("(p u) j -> p u j", u=PACK)
         out_words = out_1[0].rearrange("p c r -> p (c r)").bitcast(I32)
 
-        for u in range(PACK):
-            cols = slice(u * P, (u + 1) * P)
-            quantize(z_codes[:, cols], z_scales[:, cols], z_g[:, u, :, :])
-            if u == 0:
-                deal_z(1, 1, PACK)
-                for h in range(2):
-                    product(cv0_ps[h], z_codes, z_scales, 0, z2_codes, z2_scales, slice(h * HALF, (h + 1) * HALF))
+        def quantize_z(u):
+            features = slice(u * P, (u + 1) * P)
+            quantize(z_codes[:, features], z_scales[:, features], z_g[:, u, :, :])
+
+        quantize_z(0)
+        deal_z(1, 1, PACK)
+        for h in range(2):
+            product(cv0_ps[h], z_codes, z_scales, 0, z2_codes, z2_scales, half(h))
+        for u in range(1, PACK):
+            quantize_z(u)
+            product(cv_ps[u], z_codes, z_scales, u, z2_codes, z2_scales)
+
+        for h in range(2):
+            nc.scalar.activation(cv[0][:, half(h)], cv0_ps[h][:], ACT.Copy, scale=CV_SCALE)
+        for u in range(1, PACK):
+            nc.vector.tensor_scalar(cv[u][:, 0:H], cv_ps[u][:], CV_SCALE, None, ALU.mult)
+
+        def fetch_n4(u, h):
+            window = st[u][:].indirect(entries(n4_l, half(h)))
+            if (u, h) in N4_ON_VECTOR:
+                nc.vector.tensor_copy(st_n4[u][h][:], window)
             else:
-                product(cv_ps[u], z_codes, z_scales, u, z2_codes, z2_scales)
-
-        def leave(u):
-            if u == 0:
-                nc.scalar.activation(cv[0][:, 0:HALF], cv0_ps[0][:], ACT.Copy, scale=0.0625)
-                nc.vector.tensor_scalar(cv[0][:, HALF:H], cv0_ps[1][:], 0.0625, None, ALU.mult)
-            else:
-                nc.vector.tensor_scalar(cv[u][:, 0:H], cv_ps[u][:], 0.0625, None, ALU.mult)
-
-        def fetch3(u):
-            nc.scalar.activation(g3[u][:], cv[u][:].indirect(n3_l[:]), ACT.Copy)
-
-        def step(u):
-            nc.vector.tensor_tensor(st[u][:], cv[u][:, 0:H], g3[u][:], ALU.subtract)
-
-        def fetch4(u, h):
-            if u == 0 or (u, h) == (1, 0):
-                nc.vector.tensor_copy(g4[u][h][:], st[u][:].indirect(half_of(n4_l, h)))
-            else:
-                nc.scalar.activation(g4[u][h][:], st[u][:].indirect(half_of(n4_l, h)), ACT.Copy)
-
-        def larger(u, h):
-            cols = slice(h * HALF, (h + 1) * HALF)
-            nc.vector.tensor_tensor(y[h][:, u, :], st[u][:, cols], g4[u][h][:], ALU.max)
-            nc.sync.dma_start(out_rows[:, u, cols], y[h][:, u, :])
-
-        def hand_on(h):
-            cols = slice(h * HALF, (h + 1) * HALF)
-            quantize(y_codes[:, cols], y_scales[:, cols], y_g[h][:])
-            nc.sync.dma_start(out_words[:, cols], y_codes[:, cols])
+                nc.scalar.activation(st_n4[u][h][:], window, ACT.Copy)
 
         for u in range(PACK):
-            leave(u)
-        for u in range(PACK):
-            fetch3(u)
-            step(u)
-            if u in (1, 2):
-                fetch4(u - 1, 0)
-        fetch4(0, 1)
-        for u, h in ((2, 0), (3, 0), (1, 1), (2, 1), (3, 1)):
-            fetch4(u, h)
+            nc.scalar.activation(cv_n3[u][:], cv[u][:].indirect(n3_l[:]), ACT.Copy)
+            nc.vector.tensor_tensor(st[u][:], cv[u][:, 0:H], cv_n3[u][:], ALU.subtract)
+            if u > 0:
+                fetch_n4(*N4_ON_VECTOR[u - 1])
         for h in range(2):
             for u in range(PACK):
-                larger(u, h)
+                if (u, h) not in N4_ON_VECTOR:
+                    fetch_n4(u, h)
+        for h in range(2):
+            for u in range(PACK):
+                nc.vector.tensor_tensor(y[h][:, u, :], st[u][:, half(h)], st_n4[u][h][:], ALU.max)
+                if u % 2 == 1:
+                    nc.sync.dma_start(out_rows[:, u - 1 : u + 1, half(h)], y[h][:, u - 1 : u + 1, :])
+
         interleave(nc.scalar.copy, y_g[0][:], y[0][:])
         interleave(nc.vector.tensor_copy, y_g[1][:], y[1][:])
         for h in range(2):
-            hand_on(h)
-        for q in range(4):
-            eng = nc.scalar if q % 2 else nc.sync
-            eng.dma_start(out_2[0, 4 * q : 4 * q + 4, :].bitcast(I32), y_scales[32 * q : 32 * q + 4, :].bitcast(I32))
+            quantize(y_codes[:, half(h)], y_scales[:, half(h)], y_g[h][:])
+            nc.sync.dma_start(out_words[:, half(h)], y_codes[:, half(h)])
+        for q in range(P // QUADRANT):
+            queue = nc.scalar if q % 2 else nc.sync
+            queue.dma_start(
+                out_2[0, 4 * q : 4 * q + 4, :].bitcast(I32), y_scales[QUADRANT * q : QUADRANT * q + 4, :].bitcast(I32)
+            )

from contextlib import ExitStack

import concourse.mybir as mybir
from concourse.masks import make_identity

T, S, H = 2048, 512, 512
FLOPS = 3 * 2 * 512 * 512 * 512

F32 = mybir.dt.float32
BF16 = mybir.dt.bfloat16
I32 = mybir.dt.int32
U32 = mybir.dt.uint32
U16 = mybir.dt.uint16
U8 = mybir.dt.uint8
FP8X4 = mybir.dt.float8_e4m3fn_x4
ALU = mybir.AluOpType
ACT = mybir.ActivationFunctionType

P = 128
PACK = 4
RUN = 8
LANES = 16
QUADRANT = 32
HALF = H // 2
SPARE = 8
CV_SCALE = 0.0625
N4_ON_VECTOR = ((0, 0), (1, 0), (0, 1))


def tile_picked_momtjointbhopmx_none_po_kernel(
    tc, x_words, x_scales, wa, wb, gt, gi, offs, two, n1, n2, n3, n4, out_0, out_1, out_2
):
    nc = tc.nc
    with ExitStack() as ctx:
        keep = ctx.enter_context(tc.tile_pool(name="keep", bufs=1))
        psum = ctx.enter_context(tc.psum_pool(name="psum", bufs=1))

        def sb(name, shape, dtype, reuses=None):
            return keep.tile(shape, dtype, name=name, tag=reuses or name, align_bytes=64)

        def half(h):
            return slice(h * HALF, (h + 1) * HALF)

        def load_list(name, src):
            lst = sb(name, [P, S // LANES], U16)
            nc.sync.dma_start(lst[:], src)
            return lst

        def entries(lst, cols):
            return lst[:, cols.start // LANES : cols.stop // LANES]

        def load_weight_half(dst, w, h):
            nc.sync.dma_start(dst[:], w.rearrange("(p j) c -> p j c", j=PACK)[:, :, half(h)])

        xs = sb("xs", [P, T], U8)
        nc.vector.memset(xs[:].bitcast(I32), 0)
        gates_in = sb("gates_in", [P, P], F32)
        nc.gpsimd.memset(gates_in[:], 0.0)
        ident = sb("ident", [P, P], F32)
        make_identity(nc, ident[:])
        two_l = load_list("two_l", two)
        offs_l = load_list("offs_l", offs)
        wb_raw = [sb("wb_raw%d" % h, [P, PACK, HALF], F32) for h in range(2)]
        wa_raw = [sb("wa_raw%d" % h, [P, PACK, HALF], F32) for h in range(2)]
        load_weight_half(wb_raw[0], wb, 0)
        for q in range(P // QUADRANT):
            nc.sync.dma_start(
                xs[QUADRANT * q : QUADRANT * q + 4, :].bitcast(I32), x_scales[0, 4 * q : 4 * q + 4, :].bitcast(I32)
            )
        load_weight_half(wb_raw[1], wb, 1)
        xw = sb("xw", [P, T], I32)
        nc.sync.dma_start(xw[:], x_words[0].rearrange("p c r -> p (c r)").bitcast(I32))
        for h in range(2):
            load_weight_half(wa_raw[h], wa, h)
        for first_row, gate in ((0, gt), (PACK, gi)):
            nc.sync.dma_start(
                gates_in[first_row : first_row + PACK, :].rearrange("t (b r) -> t b r", r=RUN),
                gate.rearrange("(b t r) o -> t b (r o)", t=PACK, r=RUN),
            )
        n1_l = load_list("n1_l", n1)
        n2_l = load_list("n2_l", n2)
        n3_l = load_list("n3_l", n3)
        n4_l = load_list("n4_l", n4)

        def pick_scales(name, lst):
            gathered = sb(name + "_sg", [P, S], U8)
            nc.vector.tensor_copy(gathered[:], xs[:].indirect(lst[:]))
            dealt = sb(name + "_sd", [P, S], U8)
            nc.vector.tensor_copy(
                dealt[:].bitcast(I32).rearrange("p (t a b w) -> p a t b w", t=PACK, b=2, w=2),
                gathered[:].bitcast(I32).rearrange("p (a b t w) -> p a t b w", t=PACK, b=2, w=2),
            )
            return dealt

        def pick_words(name, lst):
            dealt = sb(name + "_wd", [P, S], I32)
            nc.vector.tensor_copy(
                dealt[:].bitcast(U32).rearrange("p (t b r) -> p b t r", t=PACK, r=RUN),
                xw[:].bitcast(U32).indirect(lst[:]),
            )
            return dealt

        def interleave(copy, dst, src):
            copy(dst.rearrange("p (c i) t -> p c t i", i=4), src.rearrange("p t (c i) -> p c t i", i=4))

        def quantize(codes, scales, grouped):
            nc.vector.quantize_mx(out=codes.bitcast(FP8X4), scales=scales, in_=grouped.rearrange("p c t -> p (c t)"))

        def product(bank, l_codes, l_scales, tile_no, r_codes, r_scales, moving=slice(0, H)):
            rows = slice(tile_no * P, (tile_no + 1) * P)
            nc.tensor.matmul_mx(
                out=bank[:],
                lhsT=l_codes[:, rows].bitcast(FP8X4),
                lhsT_scale=l_scales[:, rows],
                rhs=r_codes[:, moving].bitcast(FP8X4),
                rhs_scale=r_scales[:, moving],
                start=True,
                stop=True,
            )

        two_s = pick_scales("two", two_l)
        offs_s = pick_scales("offs", offs_l)

        wb_codes = sb("wb_codes", [P, H], U32)
        wb_scales = sb("wb_scales", [P, H], U8, "two_sg")
        wb_g = [sb("wb_g%d" % h, [P, HALF, PACK], BF16) for h in range(2)]
        for h in range(2):
            interleave(nc.scalar.copy, wb_g[h][:], wb_raw[h][:])
        for h in range(2):
            quantize(wb_codes[:, half(h)], wb_scales[:, half(h)], wb_g[h][:])

        two_w = pick_words("two", two_l)
        b0_ps = [psum.tile([P, HALF], F32, name="b0_ps%d" % h, tag=("left0", "right0")[h]) for h in range(2)]
        b_ps = {t: psum.tile([P, H], F32, name="b_ps%d" % t, tag="left%d" % t) for t in range(1, PACK)}
        b_sb = [sb("b_sb0", [P, H], F32, "wa_raw0")] + [sb("b_sb%d" % t, [P, 2 * H], F32) for t in range(1, PACK)]
        cv = [sb("cv%d" % u, [P, H + SPARE], F32) for u in range(PACK)]
        for t in range(1, PACK):
            nc.vector.memset(b_sb[t][:, H:], 0.0)
        for u in range(PACK):
            nc.vector.memset(cv[u][:, H:], 0.0)
        for h in range(2):
            product(b0_ps[h], two_w, two_s, 0, wb_codes, wb_scales, half(h))
        for t in range(1, PACK):
            product(b_ps[t], two_w, two_s, t, wb_codes, wb_scales)

        gates_ps = psum.tile([P, P], F32, name="gates_ps", tag="right1")
        nc.tensor.transpose(gates_ps[:], gates_in[:], ident[:])
        gates = sb("gates", [P, 2 * PACK], F32)
        nc.scalar.copy(gates[:], gates_ps[:, 0 : 2 * PACK])
        offs_w = pick_words("offs", offs_l)

        b_n1 = [sb("g1_%d" % t, [P, H], F32) for t in range(PACK)]
        diff = [sb("dd_%d" % t, [P, H], F32) for t in range(PACK)]
        th = [[sb("th_%d_%d" % (t, h), [P, HALF], F32) for h in range(2)] for t in range(PACK)]
        z_rows = [sb("z_rows%d" % h, [P, PACK, HALF], BF16) for h in range(2)]
        z2_rows = sb("z2_rows", [P, PACK, H], BF16)
        z_g = sb("z_g", [P, PACK, P, PACK], BF16)
        z2_g = [sb("z2_g%d" % h, [P, HALF, PACK], BF16, "dd_%d" % (2 + h)) for h in range(2)]
        z_codes = sb("z_codes", [P, H], U32)
        z_scales = sb("z_scales", [P, H], U8)
        z2_codes = sb("z2_codes", [P, H], U32)
        z2_scales = sb("z2_scales", [P, H], U8)
        wa_codes = sb("wa_codes", [P, H], U32)
        wa_scales = sb("wa_scales", [P, H], U8)
        wa_g = [sb("wa_g%d" % h, [P, HALF, PACK], BF16) for h in range(2)]
        a_ps = [psum.tile([P, H], F32, name="a_ps%d" % t, tag="right%d" % t) for t in range(PACK)]

        def difference(t, cols):
            nc.scalar.activation(b_n1[t][:, cols], b_sb[t][:].indirect(entries(n1_l, cols)), ACT.Copy)
            nc.vector.tensor_tensor(
                diff[t][:, cols], b_sb[t][:].indirect(entries(n2_l, cols)), b_n1[t][:, cols], ALU.subtract
            )

        def deal_z(h, first, last):
            nc.vector.tensor_copy(
                z_g[:, first:last, h * (P // 2) : (h + 1) * (P // 2), :].rearrange("p u (c i) t -> p c t i u", i=2),
                z_rows[h][:].rearrange("p t (c i u) -> p c t i u", i=2, u=PACK)[:, :, :, :, first:last],
            )

        interleave(nc.scalar.copy, wa_g[0][:], wa_raw[0][:])
        interleave(nc.vector.tensor_copy, wa_g[1][:], wa_raw[1][:])
        for h in range(2):
            nc.scalar.copy(b_sb[0][:, half(h)], b0_ps[h][:])
        quantize(wa_codes[:, half(0)], wa_scales[:, half(0)], wa_g[0][:])
        nc.vector.tensor_copy(b_sb[1][:, 0:H], b_ps[1][:])
        quantize(wa_codes[:, half(1)], wa_scales[:, half(1)], wa_g[1][:])
        nc.scalar.copy(b_sb[2][:, 0:H], b_ps[2][:])
        nc.vector.tensor_copy(b_sb[3][:, 0:H], b_ps[3][:])
        for t in range(PACK):
            nc.vector.tensor_scalar(
                z2_rows[:, t, :], b_sb[t][:, 0:H], gates[:, PACK + t : PACK + t + 1], None, ALU.mult
            )
        for t in range(PACK):
            product(a_ps[t], offs_w, offs_s, t, wa_codes, wa_scales)
        for h in range(2):
            difference(0, half(h))
        for t in range(1, PACK):
            difference(t, slice(0, H))
        for h in range(2):
            for t in range(PACK):
                nc.scalar.activation(th[t][h][:], diff[t][:, half(h)], ACT.Tanh, scale=-1.0)
        for h in range(2):
            interleave(nc.scalar.copy, z2_g[h][:], z2_rows[:, :, half(h)])
        for h in range(2):
            for t in range(PACK):
                nc.vector.scalar_tensor_tensor(
                    z_rows[h][:, t, :], a_ps[t][:, half(h)], gates[:, t : t + 1], th[t][h][:], ALU.mult, ALU.mult
                )
                if (t, h) == (0, 1):
                    deal_z(0, 0, PACK)
        quantize(z2_codes[:, half(0)], z2_scales[:, half(0)], z2_g[0][:])
        deal_z(1, 0, 1)
        quantize(z2_codes[:, half(1)], z2_scales[:, half(1)], z2_g[1][:])

        cv0_ps = [psum.tile([P, HALF], F32, name="cv0_ps%d" % h, tag="left%d" % h) for h in range(2)]
        cv_banks = {1: "left2", 2: "left3", 3: "right0"}
        cv_ps = {u: psum.tile([P, H], F32, name="cv_ps%d" % u, tag=cv_banks[u]) for u in range(1, PACK)}
        st = [sb("st%d" % u, [P, H], F32) for u in range(PACK)]
        cv_n3 = [sb("g3_%d" % u, [P, H], F32) for u in range(PACK)]
        st_n4 = [[sb("g4_%d_%d" % (u, h), [P, HALF], F32) for h in range(2)] for u in range(PACK)]
        y = [sb("y%d" % h, [P, PACK, HALF], F32) for h in range(2)]
        y_g = [sb("y_g%d" % h, [P, HALF, PACK], BF16) for h in range(2)]
        y_codes = sb("y_codes", [P, H], I32)
        y_scales = sb("y_scales", [P, H], U8)
        out_rows = out_0.rearrange("(p u) j -> p u j", u=PACK)
        out_words = out_1[0].rearrange("p c r -> p (c r)").bitcast(I32)

        def quantize_z(u):
            features = slice(u * P, (u + 1) * P)
            quantize(z_codes[:, features], z_scales[:, features], z_g[:, u, :, :])

        quantize_z(0)
        deal_z(1, 1, PACK)
        for h in range(2):
            product(cv0_ps[h], z_codes, z_scales, 0, z2_codes, z2_scales, half(h))
        for u in range(1, PACK):
            quantize_z(u)
            product(cv_ps[u], z_codes, z_scales, u, z2_codes, z2_scales)

        for h in range(2):
            nc.scalar.activation(cv[0][:, half(h)], cv0_ps[h][:], ACT.Copy, scale=CV_SCALE)
        for u in range(1, PACK):
            nc.vector.tensor_scalar(cv[u][:, 0:H], cv_ps[u][:], CV_SCALE, None, ALU.mult)

        def fetch_n4(u, h):
            window = st[u][:].indirect(entries(n4_l, half(h)))
            if (u, h) in N4_ON_VECTOR:
                nc.vector.tensor_copy(st_n4[u][h][:], window)
            else:
                nc.scalar.activation(st_n4[u][h][:], window, ACT.Copy)

        for u in range(PACK):
            nc.scalar.activation(cv_n3[u][:], cv[u][:].indirect(n3_l[:]), ACT.Copy)
            nc.vector.tensor_tensor(st[u][:], cv[u][:, 0:H], cv_n3[u][:], ALU.subtract)
            if u > 0:
                fetch_n4(*N4_ON_VECTOR[u - 1])
        for h in range(2):
            for u in range(PACK):
                if (u, h) not in N4_ON_VECTOR:
                    fetch_n4(u, h)
        for h in range(2):
            for u in range(PACK):
                nc.vector.tensor_tensor(y[h][:, u, :], st[u][:, half(h)], st_n4[u][h][:], ALU.max)
                if u % 2 == 1:
                    nc.sync.dma_start(out_rows[:, u - 1 : u + 1, half(h)], y[h][:, u - 1 : u + 1, :])

        interleave(nc.scalar.copy, y_g[0][:], y[0][:])
        interleave(nc.vector.tensor_copy, y_g[1][:], y[1][:])
        for h in range(2):
            quantize(y_codes[:, half(h)], y_scales[:, half(h)], y_g[h][:])
            nc.sync.dma_start(out_words[:, half(h)], y_codes[:, half(h)])
        for q in range(P // QUADRANT):
            queue = nc.scalar if q % 2 else nc.sync
            queue.dma_start(
                out_2[0, 4 * q : 4 * q + 4, :].bitcast(I32), y_scales[QUADRANT * q : QUADRANT * q + 4, :].bitcast(I32)
            )
